import numpy as np
import ml_dtypes

BF16 = ml_dtypes.bfloat16


def bf(x):
    return np.asarray(x, np.float32).astype(BF16)


def f32(x):
    return np.asarray(x, np.float32)


def f64(x):
    return np.asarray(x).astype(np.float64)


def striped(idx):
    return np.tile(idx.reshape(-1, 16).T, (8, 1))


S, K, M, N, D, V = 1024, 512, 128, 1024, 4, 256


def sigmoid(v):
    return 1.0 / (1.0 + np.exp(-v))


def setup_inputs():
    return {"table": bf(np.random.standard_normal((K, S))), "w": bf(np.random.standard_normal((K, M)) / np.sqrt(K)), "b": f32(0.5 * np.random.standard_normal((M, 1))), "offs": striped(np.random.permutation(np.tile(np.arange(S), 2))[:N])}


def reference(table, w, b, offs):
    idx = offs[:16].T.reshape(-1)
    x = f64(table)[:, idx]
    y = f64(w).T @ x
    z = (y + f64(b)) * sigmoid(y + f64(b))
    return z.reshape(M, V, D).mean(axis=2)

@@ -1,0 +1,63 @@
+import concourse.mybir as mybir
+
+BF16, F32, U16 = mybir.dt.bfloat16, mybir.dt.float32, mybir.dt.uint16
+
+P = 128
+K, S = 512, 1024
+M = 128
+N = 1024
+GROUP = 4
+KB = K // P
+PIECE = 512
+PIECES = N // PIECE
+POOLED = PIECE // GROUP
+
+FLOPS = 2 * K * M * N
+
+
+def tile_gather_matmul_kernel(tc, table, w, b, offs, out):
+    nc = tc.nc
+    with (
+        tc.tile_pool(name="held", bufs=1) as held,
+        tc.tile_pool(name="work", bufs=2) as work,
+        tc.psum_pool(name="psum", bufs=2) as psum,
+    ):
+        offsets = held.tile([P, N // 16], U16, name="offsets")
+        nc.sync.dma_start(offsets[:], offs)
+
+        weights = held.tile([P, KB, M], BF16, name="weights")
+        nc.scalar.dma_start(weights[:], w.rearrange("(kb p) m -> p kb m", p=P))
+        bias = held.tile([P, 1], F32, name="bias")
+        nc.scalar.dma_start(bias[:], b)
+
+        blocks = []
+        for kb in range(KB):
+            block = held.tile([P, S], BF16, name=f"block{kb}")
+            nc.sync.dma_start(block[:], table[kb * P : (kb + 1) * P, :])
+            blocks.append(block)
+
+        for piece in range(PIECES):
+            entries = offsets[:, piece * (PIECE // 16) : (piece + 1) * (PIECE // 16)]
+            bank = psum.tile([M, PIECE], F32, name="bank")
+            for kb in range(KB):
+                nc.tensor.matmul(
+                    bank[:],
+                    weights[:, kb, :],
+                    blocks[kb][:].indirect(entries),
+                    start=(kb == 0),
+                    stop=(kb == KB - 1),
+                )
+
+            z = work.tile([M, PIECE], F32, name="z")
+            nc.scalar.activation(z[:], bank[:], mybir.ActivationFunctionType.Silu, bias=bias[:, 0:1])
+
+            sums = work.tile([M, POOLED], F32, name="sums")
+            nc.vector.tensor_reduce(
+                sums[:],
+                z[:].rearrange("m (v t) -> m v t", t=GROUP),
+                axis=mybir.AxisListType.X,
+                op=mybir.AluOpType.add,
+            )
+            means = work.tile([M, POOLED], F32, name="means")
+            nc.vector.tensor_scalar_mul(means[:], sums[:], 1.0 / GROUP)
+            nc.sync.dma_start(out[:, piece * POOLED : (piece + 1) * POOLED], means[:])

@@ -8,56 +8,68 @@ M = 128
 N = 1024
 GROUP = 4
 KB = K // P
-PIECE = 512
-PIECES = N // PIECE
-POOLED = PIECE // GROUP
+BANK = 512
+
+WIDTHS = (256, 320, 320, 128)
+BANKS = 3
+WARM_UP = 4
 
 FLOPS = 2 * K * M * N
 
 
 def tile_gather_matmul_kernel(tc, table, w, b, offs, out):
     nc = tc.nc
+    assert sum(WIDTHS) == N
     with (
         tc.tile_pool(name="held", bufs=1) as held,
-        tc.tile_pool(name="work", bufs=2) as work,
-        tc.psum_pool(name="psum", bufs=2) as psum,
+        tc.tile_pool(name="work", bufs=len(WIDTHS)) as work,
+        tc.psum_pool(name="idle", bufs=1) as idle,
+        tc.psum_pool(name="psum", bufs=BANKS) as psum,
     ):
+        zeros = held.tile([P, BANK], BF16, name="zeros")
+        nc.vector.memset(zeros[:].bitcast(F32), 0.0)
+        idle_bank = idle.tile([M, BANK], F32, name="idle_bank")
+        for warm in range(WARM_UP):
+            nc.tensor.matmul(idle_bank[:], zeros[:, 0:M], zeros[:], start=True, stop=True)
+
         offsets = held.tile([P, N // 16], U16, name="offsets")
         nc.sync.dma_start(offsets[:], offs)
 
-        weights = held.tile([P, KB, M], BF16, name="weights")
-        nc.scalar.dma_start(weights[:], w.rearrange("(kb p) m -> p kb m", p=P))
-        bias = held.tile([P, 1], F32, name="bias")
-        nc.scalar.dma_start(bias[:], b)
-
-        blocks = []
+        weights, blocks = [], []
         for kb in range(KB):
-            block = held.tile([P, S], BF16, name=f"block{kb}")
-            nc.sync.dma_start(block[:], table[kb * P : (kb + 1) * P, :])
-            blocks.append(block)
+            rows = slice(kb * P, (kb + 1) * P)
+            weights.append(held.tile([P, M], BF16, name=f"weights{kb}"))
+            blocks.append(held.tile([P, S], BF16, name=f"block{kb}"))
+            small_queue = nc.sync if kb == 0 else nc.scalar
+            small_queue.dma_start(weights[kb][:], w[rows, :])
+            nc.scalar.dma_start(blocks[kb][:], table[rows, :])
+        bias = held.tile([P, 1], F32, name="bias")
+        nc.sync.dma_start(bias[:], b)
 
-        for piece in range(PIECES):
-            entries = offsets[:, piece * (PIECE // 16) : (piece + 1) * (PIECE // 16)]
-            bank = psum.tile([M, PIECE], F32, name="bank")
+        first = 0
+        for width in WIDTHS:
+            entries = offsets[:, first // 16 : (first + width) // 16]
+            bank = psum.tile([M, width], F32, name="bank")
             for kb in range(KB):
                 nc.tensor.matmul(
                     bank[:],
-                    weights[:, kb, :],
+                    weights[kb][:],
                     blocks[kb][:].indirect(entries),
                     start=(kb == 0),
                     stop=(kb == KB - 1),
                 )
 
-            z = work.tile([M, PIECE], F32, name="z")
+            z = work.tile([M, width], F32, name="z")
             nc.scalar.activation(z[:], bank[:], mybir.ActivationFunctionType.Silu, bias=bias[:, 0:1])
 
-            sums = work.tile([M, POOLED], F32, name="sums")
+            sums = work.tile([M, width // GROUP], F32, name="sums")
             nc.vector.tensor_reduce(
                 sums[:],
                 z[:].rearrange("m (v t) -> m v t", t=GROUP),
                 axis=mybir.AxisListType.X,
                 op=mybir.AluOpType.add,
             )
-            means = work.tile([M, POOLED], F32, name="means")
+            means = work.tile([M, width // GROUP], F32, name="means")
             nc.vector.tensor_scalar_mul(means[:], sums[:], 1.0 / GROUP)
-            nc.sync.dma_start(out[:, piece * POOLED : (piece + 1) * POOLED], means[:])
+            nc.sync.dma_start(out[:, first // GROUP : (first + width) // GROUP], means[:])
+            first += width

@@ -1,6 +1,7 @@
 import concourse.mybir as mybir
 
 BF16, F32, U16 = mybir.dt.bfloat16, mybir.dt.float32, mybir.dt.uint16
+SILU = mybir.ActivationFunctionType.Silu
 
 P = 128
 K, S = 512, 1024
@@ -8,11 +9,9 @@ M = 128
 N = 1024
 GROUP = 4
 KB = K // P
-BANK = 512
 
 WIDTHS = (256, 320, 320, 128)
 BANKS = 3
-WARM_UP = 4
 
 FLOPS = 2 * K * M * N
 
@@ -23,14 +22,12 @@ def tile_gather_matmul_kernel(tc, table, w, b, offs, out):
     with (
         tc.tile_pool(name="held", bufs=1) as held,
         tc.tile_pool(name="work", bufs=len(WIDTHS)) as work,
-        tc.psum_pool(name="idle", bufs=1) as idle,
         tc.psum_pool(name="psum", bufs=BANKS) as psum,
     ):
-        zeros = held.tile([P, BANK], BF16, name="zeros")
-        nc.vector.memset(zeros[:].bitcast(F32), 0.0)
-        idle_bank = idle.tile([M, BANK], F32, name="idle_bank")
-        for warm in range(WARM_UP):
-            nc.tensor.matmul(idle_bank[:], zeros[:, 0:M], zeros[:], start=True, stop=True)
+        nothing = held.tile([P, 1], F32, name="nothing")
+        nc.vector.memset(nothing[:], 0.0)
+        unused = held.tile([P, 1], F32, name="unused")
+        nc.scalar.activation(unused[:], nothing[:], SILU)
 
         offsets = held.tile([P, N // 16], U16, name="offsets")
         nc.sync.dma_start(offsets[:], offs)
@@ -44,7 +41,7 @@ def tile_gather_matmul_kernel(tc, table, w, b, offs, out):
             small_queue.dma_start(weights[kb][:], w[rows, :])
             nc.scalar.dma_start(blocks[kb][:], table[rows, :])
         bias = held.tile([P, 1], F32, name="bias")
-        nc.sync.dma_start(bias[:], b)
+        nc.scalar.dma_start(bias[:], b)
 
         first = 0
         for width in WIDTHS:
@@ -60,7 +57,7 @@ def tile_gather_matmul_kernel(tc, table, w, b, offs, out):
                 )
 
             z = work.tile([M, width], F32, name="z")
-            nc.scalar.activation(z[:], bank[:], mybir.ActivationFunctionType.Silu, bias=bias[:, 0:1])
+            nc.scalar.activation(z[:], bank[:], SILU, bias=bias[:, 0:1])
 
             sums = work.tile([M, width // GROUP], F32, name="sums")
             nc.vector.tensor_reduce(

@@ -24,11 +24,6 @@ def tile_gather_matmul_kernel(tc, table, w, b, offs, out):
         tc.tile_pool(name="work", bufs=len(WIDTHS)) as work,
         tc.psum_pool(name="psum", bufs=BANKS) as psum,
     ):
-        nothing = held.tile([P, 1], F32, name="nothing")
-        nc.vector.memset(nothing[:], 0.0)
-        unused = held.tile([P, 1], F32, name="unused")
-        nc.scalar.activation(unused[:], nothing[:], SILU)
-
         offsets = held.tile([P, N // 16], U16, name="offsets")
         nc.sync.dma_start(offsets[:], offs)
 

@@ -27,6 +27,7 @@ def tile_gather_matmul_kernel(tc, table, w, b, offs, out):
         offsets = held.tile([P, N // 16], U16, name="offsets")
         nc.sync.dma_start(offsets[:], offs)
 
+        bias = held.tile([P, 1], F32, name="bias")
         weights, blocks = [], []
         for kb in range(KB):
             rows = slice(kb * P, (kb + 1) * P)
@@ -35,8 +36,8 @@ def tile_gather_matmul_kernel(tc, table, w, b, offs, out):
             small_queue = nc.sync if kb == 0 else nc.scalar
             small_queue.dma_start(weights[kb][:], w[rows, :])
             nc.scalar.dma_start(blocks[kb][:], table[rows, :])
-        bias = held.tile([P, 1], F32, name="bias")
-        nc.scalar.dma_start(bias[:], b)
+            if kb == 0:
+                nc.scalar.dma_start(bias[:], b)
 
         first = 0
         for width in WIDTHS:

@@ -27,7 +27,6 @@ def tile_gather_matmul_kernel(tc, table, w, b, offs, out):
         offsets = held.tile([P, N // 16], U16, name="offsets")
         nc.sync.dma_start(offsets[:], offs)
 
-        bias = held.tile([P, 1], F32, name="bias")
         weights, blocks = [], []
         for kb in range(KB):
             rows = slice(kb * P, (kb + 1) * P)
@@ -36,8 +35,13 @@ def tile_gather_matmul_kernel(tc, table, w, b, offs, out):
             small_queue = nc.sync if kb == 0 else nc.scalar
             small_queue.dma_start(weights[kb][:], w[rows, :])
             nc.scalar.dma_start(blocks[kb][:], table[rows, :])
-            if kb == 0:
-                nc.scalar.dma_start(bias[:], b)
+
+        lying = held.tile([P, 32], F32, name="lying", align_bytes=64)
+        nc.vector.memset(lying[:], 0.0)
+        nc.sync.dma_start(lying[0:P:32, :], b.rearrange("(q c) o -> q (c o)", c=32))
+        upright = held.tile([P, 32], F32, name="upright", align_bytes=64)
+        nc.vector.transpose(upright[:], lying[:])
+        bias = upright[:, 0:1]
 
         first = 0
         for width in WIDTHS:
@@ -53,7 +57,7 @@ def tile_gather_matmul_kernel(tc, table, w, b, offs, out):
                 )
 
             z = work.tile([M, width], F32, name="z")
-            nc.scalar.activation(z[:], bank[:], SILU, bias=bias[:, 0:1])
+            nc.scalar.activation(z[:], bank[:], SILU, bias=bias)
 
             sums = work.tile([M, width // GROUP], F32, name="sums")
             nc.vector.tensor_reduce(

@@ -25,8 +25,6 @@ def tile_gather_matmul_kernel(tc, table, w, b, offs, out):
         tc.psum_pool(name="psum", bufs=BANKS) as psum,
     ):
         offsets = held.tile([P, N // 16], U16, name="offsets")
-        nc.sync.dma_start(offsets[:], offs)
-
         weights, blocks = [], []
         for kb in range(KB):
             rows = slice(kb * P, (kb + 1) * P)
@@ -35,6 +33,8 @@ def tile_gather_matmul_kernel(tc, table, w, b, offs, out):
             small_queue = nc.sync if kb == 0 else nc.scalar
             small_queue.dma_start(weights[kb][:], w[rows, :])
             nc.scalar.dma_start(blocks[kb][:], table[rows, :])
+            if kb == 0:
+                nc.sync.dma_start(offsets[:], offs)
 
         lying = held.tile([P, 32], F32, name="lying", align_bytes=64)
         nc.vector.memset(lying[:], 0.0)

import concourse.mybir as mybir

BF16, F32, U16 = mybir.dt.bfloat16, mybir.dt.float32, mybir.dt.uint16
SILU = mybir.ActivationFunctionType.Silu

P = 128
K, S = 512, 1024
M = 128
N = 1024
GROUP = 4
KB = K // P

WIDTHS = (256, 320, 320, 128)
BANKS = 3

FLOPS = 2 * K * M * N


def tile_gather_matmul_kernel(tc, table, w, b, offs, out):
    nc = tc.nc
    assert sum(WIDTHS) == N
    with (
        tc.tile_pool(name="held", bufs=1) as held,
        tc.tile_pool(name="work", bufs=len(WIDTHS)) as work,
        tc.psum_pool(name="psum", bufs=BANKS) as psum,
    ):
        offsets = held.tile([P, N // 16], U16, name="offsets")
        weights, blocks = [], []
        for kb in range(KB):
            rows = slice(kb * P, (kb + 1) * P)
            weights.append(held.tile([P, M], BF16, name=f"weights{kb}"))
            blocks.append(held.tile([P, S], BF16, name=f"block{kb}"))
            small_queue = nc.sync if kb == 0 else nc.scalar
            small_queue.dma_start(weights[kb][:], w[rows, :])
            nc.scalar.dma_start(blocks[kb][:], table[rows, :])
            if kb == 0:
                nc.sync.dma_start(offsets[:], offs)

        lying = held.tile([P, 32], F32, name="lying", align_bytes=64)
        nc.vector.memset(lying[:], 0.0)
        nc.sync.dma_start(lying[0:P:32, :], b.rearrange("(q c) o -> q (c o)", c=32))
        upright = held.tile([P, 32], F32, name="upright", align_bytes=64)
        nc.vector.transpose(upright[:], lying[:])
        bias = upright[:, 0:1]

        first = 0
        for width in WIDTHS:
            entries = offsets[:, first // 16 : (first + width) // 16]
            bank = psum.tile([M, width], F32, name="bank")
            for kb in range(KB):
                nc.tensor.matmul(
                    bank[:],
                    weights[kb][:],
                    blocks[kb][:].indirect(entries),
                    start=(kb == 0),
                    stop=(kb == KB - 1),
                )

            z = work.tile([M, width], F32, name="z")
            nc.scalar.activation(z[:], bank[:], SILU, bias=bias)

            sums = work.tile([M, width // GROUP], F32, name="sums")
            nc.vector.tensor_reduce(
                sums[:],
                z[:].rearrange("m (v t) -> m v t", t=GROUP),
                axis=mybir.AxisListType.X,
                op=mybir.AluOpType.add,
            )
            means = work.tile([M, width // GROUP], F32, name="means")
            nc.vector.tensor_scalar_mul(means[:], sums[:], 1.0 / GROUP)
            nc.sync.dma_start(out[:, first // GROUP : (first + width) // GROUP], means[:])
            first += width
